import numpy as np
import ml_dtypes


def mxq(x, axis, fmt="e4m3"):
    dtype, down = {"e4m3": (ml_dtypes.float8_e4m3fn, 7), "e5m2": (ml_dtypes.float8_e5m2, 14)}[fmt]
    v = np.moveaxis(np.asarray(x, np.float32).astype(ml_dtypes.bfloat16).astype(np.float64), axis, -1)
    blocks = v.reshape(v.shape[:-1] + (-1, 32))
    amax = np.abs(blocks).max(-1, keepdims=True)
    byte = np.maximum(np.where(amax > 0, np.frexp(amax)[1] - 1 + 127, 0) - down, 1)
    scale = np.exp2(byte - 127.0)
    codes = (blocks / scale).astype(np.float32).astype(dtype).astype(np.float64)
    return np.moveaxis((codes * scale).reshape(v.shape), -1, axis)


WIDE = False


def mx_kscale(k):
    if not WIDE:
        return np.ones(k)
    levels = np.array([10, -10, 5, -5, 0])
    if k % 512:
        return np.exp2(np.random.permutation(np.resize(levels, k // 32))).repeat(32)
    a = np.empty((k // 512, 16))
    for p in range(k // 512):
        a[p, :8] = np.random.permutation(np.resize(levels, 8))
        for g in range(8):
            far = levels[np.abs(levels - a[p, g]) >= 10]
            a[p, g + 8] = far[np.random.randint(len(far))]
    return np.exp2(a.ravel()).repeat(32)


def f64(x):
    return np.asarray(x).astype(np.float64)


def striped8(idx):
    return np.asarray(idx).reshape(8, -1, 16).transpose(0, 2, 1).reshape(128, -1).astype(np.uint16)


def unstriped8(offs):
    return offs.reshape(8, 16, -1).transpose(0, 2, 1).reshape(8, -1).astype(np.int64)


def pick8(x, idx, run):
    r = np.arange(len(x))
    return x[r[:, None], idx[r % (8 * run) // run]]


E2M1 = np.array([0.0, 0.5, 1.0, 1.5, 2.0, 3.0, 4.0, 6.0, -0.0, -0.5, -1.0, -1.5, -2.0, -3.0, -4.0, -6.0])


def pack_weight(w, fmt):
    k, n = w.shape
    w = f64(np.asarray(w, np.float32).astype(ml_dtypes.bfloat16)).reshape(k // 32, 32, n)
    amax = np.abs(w).max(1)
    if fmt == "e4m3":
        byte = np.frexp(amax)[1] - 1 + 127 - 7
    else:
        mant, ex = np.frexp(amax / 6.0)
        byte = np.where(mant > 0.5, ex, ex - 1) + 127
    byte = np.clip(np.where(amax > 0, byte, 1), 1, 254)
    scaled = (w * np.exp2(127.0 - byte)[:, None, :]).reshape(k, n).astype(np.float32)
    by_word = np.ascontiguousarray(scaled.reshape(k // 512, 128, 4, n).transpose(0, 1, 3, 2))
    if fmt == "e4m3":
        words = by_word.astype(ml_dtypes.float8_e4m3fn).view(np.uint8)
    else:
        c = by_word.astype(ml_dtypes.float4_e2m1fn).view(np.uint8) & 0xF
        words = (c[..., 0::2] | (c[..., 1::2] << 4)).reshape(k // 512, 128, 2 * n)
    return np.ascontiguousarray(words), np.ascontiguousarray(byte.astype(np.uint8).reshape(k // 512, 16, n))


def unpack_weight(words, scales, fmt):
    g, _, n = scales.shape
    words = np.ascontiguousarray(words).reshape(g, 128, n, -1)
    if fmt == "e4m3":
        vals = words.view(ml_dtypes.float8_e4m3fn).astype(np.float64)
    else:
        nib = np.empty((g, 128, n, 4), np.uint8)
        nib[..., 0::2] = words & 0xF
        nib[..., 1::2] = words >> 4
        vals = E2M1[nib]
    vals = vals * np.repeat(np.exp2(scales.astype(np.float64) - 127.0), 8, axis=1)[..., None]
    return vals.transpose(0, 1, 3, 2).reshape(g * 512, n)


D, T, U, Z, I, Q = 512, 1024, 1024, 1024, 512, 128


def setup_inputs():
    n = np.random.standard_normal
    idx = np.stack([np.random.permutation(T)[:I] for _ in range(8)])
    idx2 = np.stack([np.random.permutation(U)[:I] for _ in range(8)])
    idx3 = np.stack([np.random.permutation(Z)[:I] for _ in range(8)])
    idx4 = np.stack([np.random.permutation(Z)[:I] for _ in range(8)])
    idx5 = np.stack([np.random.permutation(Z)[:I] for _ in range(8)])
    fd = mx_kscale(D)
    keysp = pack_weight(n((D, T)) / fd[:, None], "e2m1")
    notesp = pack_weight(n((D, U)) / fd[:, None], "e4m3")
    return {
        "query": (n((D, Q)) * 1.0 / np.sqrt(D) * fd[:, None]).astype(np.float32),
        "keys_words": keysp[0],
        "keys_scales": keysp[1],
        "notes_words": notesp[0],
        "notes_scales": notesp[1],
        "lam": (np.random.uniform(0.5, 1.5, (Q, 1))).astype(np.float32),
        "offs": striped8(idx),
        "offs2": striped8(idx2),
        "offs3": striped8(idx3),
        "offs4": striped8(idx4),
        "offs5": striped8(idx5),
    }


def reference(query, keys_words, keys_scales, notes_words, notes_scales, lam, offs, offs2, offs3, offs4, offs5):
    idx = unstriped8(offs)
    idx2 = unstriped8(offs2)
    idx3 = unstriped8(offs3)
    idx4 = unstriped8(offs4)
    idx5 = unstriped8(offs5)
    keysu = unpack_weight(keys_words, keys_scales, "e2m1")
    notesu = unpack_weight(notes_words, notes_scales, "e4m3")
    queryq = mxq(f64(query), 0, "e4m3")
    a = queryq.T @ keysu
    b = queryq.T @ notesu
    ta = np.max(a, axis=1, keepdims=True)
    tb = np.max(b, axis=1, keepdims=True)
    e1 = np.exp(pick8(a, idx, 16) - ta)
    e2 = np.exp(pick8(b, idx2, 16) - tb)
    f1 = np.zeros((Q, Z))
    f1[np.arange(Q)[:, None], idx3[np.arange(Q) % 128 // 16]] = e1
    f2 = np.zeros((Q, Z))
    f2[np.arange(Q)[:, None], idx4[np.arange(Q) % 128 // 16]] = e2
    cc = f1 + f2 * f64(lam)
    y = pick8(cc, idx5, 16) * 8.0
    return y

@@ -1,0 +1,114 @@
+from contextlib import ExitStack
+
+import concourse.mybir as mybir
+
+F32 = mybir.dt.float32
+BF16 = mybir.dt.bfloat16
+I32 = mybir.dt.int32
+U32 = mybir.dt.uint32
+U16 = mybir.dt.uint16
+U8 = mybir.dt.uint8
+FP8X4 = mybir.dt.float8_e4m3fn_x4
+FP4X4 = mybir.dt.float4_e2m1fn_x4
+ALU = mybir.AluOpType
+ACT = mybir.ActivationFunctionType
+
+P = 128
+PACK = 4
+D, Q, POOL, PLACES, SLOTS = 512, 128, 1024, 1024, 512
+BANK = 512
+HALF = SLOTS // 2
+GROUP = 16
+
+FLOPS = 2 * D * Q * 2 * POOL
+
+
+def half_of_list(lst, h):
+    return lst[:, h * HALF // GROUP : (h + 1) * HALF // GROUP]
+
+
+def tile_attend_fusedvotes_two_kernel(tc, query, keys_words, keys_scales, notes_words, notes_scales, lam,
+                                       offs, offs2, offs3, offs4, offs5, out):
+    nc = tc.nc
+    with ExitStack() as ctx:
+        sb = ctx.enter_context(tc.tile_pool(name="sb", bufs=1))
+        ps = ctx.enter_context(tc.psum_pool(name="ps", bufs=1))
+
+        k_scale = sb.tile([P, POOL], U8, name="k_scale", align_bytes=64)
+        n_scale = sb.tile([P, POOL], U8, name="n_scale", align_bytes=64)
+        f1 = sb.tile([P, PLACES], F32, name="f1")
+        f2 = sb.tile([P, PLACES], F32, name="f2")
+        nc.vector.memset(f1[:], 0.0)
+        nc.vector.memset(f2[:], 0.0)
+
+        q_raw = sb.tile([P, PACK, Q], F32, name="q_raw")
+        k_words = sb.tile([P, 2 * POOL], U8, name="k_words", align_bytes=64)
+        n_words = sb.tile([P, POOL], U32, name="n_words", align_bytes=64)
+        lam_sb = sb.tile([P, 1], F32, name="lam_sb")
+        lists = [sb.tile([P, SLOTS // GROUP], U16, name="list%d" % j) for j in range(5)]
+
+        def load_scales(plane, scales):
+            for c in range(4):
+                nc.sync.dma_start(out=plane[32 * c : 32 * c + 4, :].bitcast(I32),
+                                  in_=scales[0, 4 * c : 4 * c + 4, :].bitcast(I32))
+
+        nc.sync.dma_start(out=q_raw[:], in_=query.rearrange("(p t) q -> p t q", t=PACK))
+        load_scales(k_scale, keys_scales)
+        nc.sync.dma_start(out=k_words[:].bitcast(I32), in_=keys_words[0].bitcast(I32))
+        nc.sync.dma_start(lists[0][:], offs)
+        nc.sync.dma_start(out=n_words[:].bitcast(I32),
+                          in_=notes_words[0].rearrange("p n t -> p (n t)").bitcast(I32))
+        load_scales(n_scale, notes_scales)
+        nc.sync.dma_start(lists[2][:], offs3)
+        nc.sync.dma_start(lists[1][:], offs2)
+        nc.sync.dma_start(lists[3][:], offs4)
+        nc.sync.dma_start(lists[4][:], offs5)
+        nc.sync.dma_start(out=lam_sb[:], in_=lam)
+
+        q_bf = sb.tile([P, Q, PACK], BF16, name="q_bf", align_bytes=64)
+        q_words = sb.tile([P, Q], U32, name="q_words", align_bytes=64)
+        q_scale = sb.tile([P, Q], U8, name="q_scale", align_bytes=64)
+        nc.vector.tensor_copy(out=q_bf[:], in_=q_raw[:].rearrange("p t q -> p q t"))
+        nc.vector.quantize_mx(out=q_words[:].bitcast(FP8X4), scales=q_scale[:],
+                              in_=q_bf[:].rearrange("p q t -> p (q t)"))
+
+        def score(name, moving, scale):
+            rows = sb.tile([P, POOL], F32, name=name + "_rows")
+            tops = sb.tile([P, POOL // BANK], F32, name=name + "_tops")
+            neg = sb.tile([P, 1], F32, name=name + "_neg")
+            for j in range(POOL // BANK):
+                cols = slice(j * BANK, (j + 1) * BANK)
+                bank = ps.tile([P, BANK], F32, name="%s_bank%d" % (name, j))
+                nc.tensor.matmul_mx(out=bank[:], lhsT=q_words[:].bitcast(FP8X4), lhsT_scale=q_scale[:],
+                                    rhs=moving(j), rhs_scale=scale[:, cols], start=True, stop=True)
+                nc.vector.tensor_scalar(out=rows[:, cols], in0=bank[:], scalar1=1.0, scalar2=None,
+                                        op0=ALU.mult, op1=ALU.max, accum_out=tops[:, j : j + 1])
+            nc.gpsimd.tensor_scalar(out=neg[:], in0=tops[:, 0:1], scalar1=tops[:, 1:2], scalar2=-1.0,
+                                    op0=ALU.max, op1=ALU.mult)
+            return rows, neg
+
+        a, neg_ta = score("a", lambda j: k_words[:, 2 * j * BANK : 2 * (j + 1) * BANK].bitcast(FP4X4), k_scale)
+        b, neg_tb = score("b", lambda j: n_words[:, j * BANK : (j + 1) * BANK].bitcast(FP8X4), n_scale)
+
+        def vote(name, rows, neg, fetch, place, votes):
+            for h in range(2):
+                e = sb.tile([P, HALF], F32, name="%s_%d" % (name, h))
+                nc.scalar.activation(e[:], rows[:].indirect(half_of_list(fetch, h)), ACT.Exp, bias=neg[:])
+                nc.vector.tensor_copy(votes[:].indirect(half_of_list(place, h)), e[:])
+
+        vote("e1", a, neg_ta, lists[0], lists[2], f1)
+        e2 = sb.tile([P, SLOTS], F32, name="e2")
+        nc.scalar.activation(e2[:], b[:].indirect(lists[1][:]), ACT.Exp, bias=neg_tb[:])
+        nc.vector.tensor_copy(f2[:].indirect(lists[3][:]), e2[:])
+
+        cc = sb.tile([P, PLACES], F32, name="cc")
+        nc.vector.scalar_tensor_tensor(out=cc[:], in0=f2[:], scalar=lam_sb[:], in1=f1[:],
+                                       op0=ALU.mult, op1=ALU.add)
+
+        y0 = sb.tile([P, HALF], F32, name="y0")
+        y1 = sb.tile([P, HALF], F32, name="y1")
+        nc.vector.tensor_scalar(out=y0[:], in0=cc[:].indirect(half_of_list(lists[4], 0)), scalar1=8.0,
+                                scalar2=0.0, op0=ALU.mult, op1=ALU.add)
+        nc.scalar.activation(y1[:], cc[:].indirect(half_of_list(lists[4], 1)), ACT.Copy, scale=8.0)
+        nc.sync.dma_start(out=out[:, 0:HALF], in_=y0[:])
+        nc.scalar.dma_start(out=out[:, HALF:SLOTS], in_=y1[:])

@@ -16,7 +16,6 @@ ACT = mybir.ActivationFunctionType
 P = 128
 PACK = 4
 D, Q, POOL, PLACES, SLOTS = 512, 128, 1024, 1024, 512
-BANK = 512
 HALF = SLOTS // 2
 GROUP = 16
 
@@ -25,6 +24,11 @@ FLOPS = 2 * D * Q * 2 * POOL
 
 def half_of_list(lst, h):
     return lst[:, h * HALF // GROUP : (h + 1) * HALF // GROUP]
+
+
+def load_scale_rows(queue, plane, scales, c):
+    queue.dma_start(out=plane[32 * c : 32 * c + 4, :].bitcast(I32),
+                    in_=scales[0, 4 * c : 4 * c + 4, :].bitcast(I32))
 
 
 def tile_attend_fusedvotes_two_kernel(tc, query, keys_words, keys_scales, notes_words, notes_scales, lam,
@@ -40,6 +44,8 @@ def tile_attend_fusedvotes_two_kernel(tc, query, keys_words, keys_scales, notes_
         f2 = sb.tile([P, PLACES], F32, name="f2")
         nc.vector.memset(f1[:], 0.0)
         nc.vector.memset(f2[:], 0.0)
+        eights = sb.tile([P, 192], F32, name="eights")
+        nc.gpsimd.memset(eights[:], 8.0)
 
         q_raw = sb.tile([P, PACK, Q], F32, name="q_raw")
         k_words = sb.tile([P, 2 * POOL], U8, name="k_words", align_bytes=64)
@@ -47,20 +53,21 @@ def tile_attend_fusedvotes_two_kernel(tc, query, keys_words, keys_scales, notes_
         lam_sb = sb.tile([P, 1], F32, name="lam_sb")
         lists = [sb.tile([P, SLOTS // GROUP], U16, name="list%d" % j) for j in range(5)]
 
-        def load_scales(plane, scales):
-            for c in range(4):
-                nc.sync.dma_start(out=plane[32 * c : 32 * c + 4, :].bitcast(I32),
-                                  in_=scales[0, 4 * c : 4 * c + 4, :].bitcast(I32))
-
         nc.sync.dma_start(out=q_raw[:], in_=query.rearrange("(p t) q -> p t q", t=PACK))
-        load_scales(k_scale, keys_scales)
+        load_scale_rows(nc.sync, k_scale, keys_scales, 0)
+        load_scale_rows(nc.sync, k_scale, keys_scales, 1)
+        load_scale_rows(nc.sync, k_scale, keys_scales, 2)
+        load_scale_rows(nc.sync, k_scale, keys_scales, 3)
         nc.sync.dma_start(out=k_words[:].bitcast(I32), in_=keys_words[0].bitcast(I32))
-        nc.sync.dma_start(lists[0][:], offs)
         nc.sync.dma_start(out=n_words[:].bitcast(I32),
                           in_=notes_words[0].rearrange("p n t -> p (n t)").bitcast(I32))
-        load_scales(n_scale, notes_scales)
-        nc.sync.dma_start(lists[2][:], offs3)
+        load_scale_rows(nc.sync, n_scale, notes_scales, 0)
+        load_scale_rows(nc.sync, n_scale, notes_scales, 1)
+        load_scale_rows(nc.sync, n_scale, notes_scales, 2)
+        load_scale_rows(nc.sync, n_scale, notes_scales, 3)
+        nc.sync.dma_start(lists[0][:], offs)
         nc.sync.dma_start(lists[1][:], offs2)
+        nc.sync.dma_start(lists[2][:], offs3)
         nc.sync.dma_start(lists[3][:], offs4)
         nc.sync.dma_start(lists[4][:], offs5)
         nc.sync.dma_start(out=lam_sb[:], in_=lam)
@@ -68,47 +75,48 @@ def tile_attend_fusedvotes_two_kernel(tc, query, keys_words, keys_scales, notes_
         q_bf = sb.tile([P, Q, PACK], BF16, name="q_bf", align_bytes=64)
         q_words = sb.tile([P, Q], U32, name="q_words", align_bytes=64)
         q_scale = sb.tile([P, Q], U8, name="q_scale", align_bytes=64)
-        nc.vector.tensor_copy(out=q_bf[:], in_=q_raw[:].rearrange("p t q -> p q t"))
+        nc.vector.tensor_copy(out=q_bf[:, 0:64, :], in_=q_raw[:, :, 0:64].rearrange("p t q -> p q t"))
+        nc.scalar.copy(out=q_bf[:, 64:Q, :], in_=q_raw[:, :, 64:Q].rearrange("p t q -> p q t"))
         nc.vector.quantize_mx(out=q_words[:].bitcast(FP8X4), scales=q_scale[:],
                               in_=q_bf[:].rearrange("p q t -> p (q t)"))
 
-        def score(name, moving, scale):
+        def score(name, moving, scale, widths):
             rows = sb.tile([P, POOL], F32, name=name + "_rows")
-            tops = sb.tile([P, POOL // BANK], F32, name=name + "_tops")
+            tops = sb.tile([P, len(widths)], F32, name=name + "_tops", tag=name + "_tops")
             neg = sb.tile([P, 1], F32, name=name + "_neg")
-            for j in range(POOL // BANK):
-                cols = slice(j * BANK, (j + 1) * BANK)
-                bank = ps.tile([P, BANK], F32, name="%s_bank%d" % (name, j))
+            lo = 0
+            for j, width in enumerate(widths):
+                bank = ps.tile([P, width], F32, name="%s_bank%d" % (name, j))
                 nc.tensor.matmul_mx(out=bank[:], lhsT=q_words[:].bitcast(FP8X4), lhsT_scale=q_scale[:],
-                                    rhs=moving(j), rhs_scale=scale[:, cols], start=True, stop=True)
-                nc.vector.tensor_scalar(out=rows[:, cols], in0=bank[:], scalar1=1.0, scalar2=None,
+                                    rhs=moving(lo, lo + width), rhs_scale=scale[:, lo : lo + width],
+                                    start=True, stop=True)
+                nc.vector.tensor_scalar(out=rows[:, lo : lo + width], in0=bank[:], scalar1=1.0,
+                                        scalar2=tops[:, j - 2 : j - 1] if j >= 2 else None,
                                         op0=ALU.mult, op1=ALU.max, accum_out=tops[:, j : j + 1])
-            nc.gpsimd.tensor_scalar(out=neg[:], in0=tops[:, 0:1], scalar1=tops[:, 1:2], scalar2=-1.0,
-                                    op0=ALU.max, op1=ALU.mult)
+                lo = lo + width
+            n = len(widths)
+            nc.gpsimd.tensor_scalar(out=neg[:], in0=tops[:, n - 2 : n - 1], scalar1=tops[:, n - 1 : n],
+                                    scalar2=-1.0, op0=ALU.max, op1=ALU.mult)
             return rows, neg
 
-        a, neg_ta = score("a", lambda j: k_words[:, 2 * j * BANK : 2 * (j + 1) * BANK].bitcast(FP4X4), k_scale)
-        b, neg_tb = score("b", lambda j: n_words[:, j * BANK : (j + 1) * BANK].bitcast(FP8X4), n_scale)
+        a, neg_ta = score("a", lambda lo, hi: k_words[:, 2 * lo : 2 * hi].bitcast(FP4X4), k_scale, (256, 256, 512))
+        b, neg_tb = score("b", lambda lo, hi: n_words[:, lo:hi].bitcast(FP8X4), n_scale, (512, 512))
 
-        def vote(name, rows, neg, fetch, place, votes):
-            for h in range(2):
-                e = sb.tile([P, HALF], F32, name="%s_%d" % (name, h))
-                nc.scalar.activation(e[:], rows[:].indirect(half_of_list(fetch, h)), ACT.Exp, bias=neg[:])
-                nc.vector.tensor_copy(votes[:].indirect(half_of_list(place, h)), e[:])
-
-        vote("e1", a, neg_ta, lists[0], lists[2], f1)
-        e2 = sb.tile([P, SLOTS], F32, name="e2")
-        nc.scalar.activation(e2[:], b[:].indirect(lists[1][:]), ACT.Exp, bias=neg_tb[:])
-        nc.vector.tensor_copy(f2[:].indirect(lists[3][:]), e2[:])
+        for h in range(2):
+            e1 = sb.tile([P, HALF], F32, name="e1_%d" % h, tag="b_tops" if h == 1 else "e1_first")
+            nc.scalar.activation(e1[:], a[:].indirect(half_of_list(lists[0], h)), ACT.Exp, bias=neg_ta[:])
+            nc.vector.tensor_copy(f1[:].indirect(half_of_list(lists[2], h)), e1[:])
+            e2 = sb.tile([P, HALF], F32, name="e2_%d" % h)
+            nc.scalar.activation(e2[:], b[:].indirect(half_of_list(lists[1], h)), ACT.Exp, bias=neg_tb[:])
+            nc.vector.tensor_copy(f2[:].indirect(half_of_list(lists[3], h)), e2[:])
 
         cc = sb.tile([P, PLACES], F32, name="cc")
         nc.vector.scalar_tensor_tensor(out=cc[:], in0=f2[:], scalar=lam_sb[:], in1=f1[:],
                                        op0=ALU.mult, op1=ALU.add)
 
-        y0 = sb.tile([P, HALF], F32, name="y0")
-        y1 = sb.tile([P, HALF], F32, name="y1")
-        nc.vector.tensor_scalar(out=y0[:], in0=cc[:].indirect(half_of_list(lists[4], 0)), scalar1=8.0,
-                                scalar2=0.0, op0=ALU.mult, op1=ALU.add)
-        nc.scalar.activation(y1[:], cc[:].indirect(half_of_list(lists[4], 1)), ACT.Copy, scale=8.0)
-        nc.sync.dma_start(out=out[:, 0:HALF], in_=y0[:])
-        nc.scalar.dma_start(out=out[:, HALF:SLOTS], in_=y1[:])
+        y0 = sb.tile([P, 192], F32, name="y0")
+        y1 = sb.tile([P, SLOTS - 192], F32, name="y1")
+        nc.vector.tensor_tensor(y0[:], cc[:].indirect(lists[4][:, 0 : 192 // GROUP]), eights[:], ALU.mult)
+        nc.scalar.activation(y1[:], cc[:].indirect(lists[4][:, 192 // GROUP : SLOTS // GROUP]), ACT.Copy, scale=8.0)
+        nc.sync.dma_start(out=out[:, 0:192], in_=y0[:])
+        nc.scalar.dma_start(out=out[:, 192:SLOTS], in_=y1[:])

from contextlib import ExitStack

import concourse.mybir as mybir

F32 = mybir.dt.float32
BF16 = mybir.dt.bfloat16
I32 = mybir.dt.int32
U32 = mybir.dt.uint32
U16 = mybir.dt.uint16
U8 = mybir.dt.uint8
FP8X4 = mybir.dt.float8_e4m3fn_x4
FP4X4 = mybir.dt.float4_e2m1fn_x4
ALU = mybir.AluOpType
ACT = mybir.ActivationFunctionType

P = 128
PACK = 4
D, Q, POOL, PLACES, SLOTS = 512, 128, 1024, 1024, 512
HALF = SLOTS // 2
GROUP = 16

FLOPS = 2 * D * Q * 2 * POOL


def half_of_list(lst, h):
    return lst[:, h * HALF // GROUP : (h + 1) * HALF // GROUP]


def load_scale_rows(queue, plane, scales, c):
    queue.dma_start(out=plane[32 * c : 32 * c + 4, :].bitcast(I32),
                    in_=scales[0, 4 * c : 4 * c + 4, :].bitcast(I32))


def tile_attend_fusedvotes_two_kernel(tc, query, keys_words, keys_scales, notes_words, notes_scales, lam,
                                       offs, offs2, offs3, offs4, offs5, out):
    nc = tc.nc
    with ExitStack() as ctx:
        sb = ctx.enter_context(tc.tile_pool(name="sb", bufs=1))
        ps = ctx.enter_context(tc.psum_pool(name="ps", bufs=1))

        k_scale = sb.tile([P, POOL], U8, name="k_scale", align_bytes=64)
        n_scale = sb.tile([P, POOL], U8, name="n_scale", align_bytes=64)
        f1 = sb.tile([P, PLACES], F32, name="f1")
        f2 = sb.tile([P, PLACES], F32, name="f2")
        nc.vector.memset(f1[:], 0.0)
        nc.vector.memset(f2[:], 0.0)
        eights = sb.tile([P, 192], F32, name="eights")
        nc.gpsimd.memset(eights[:], 8.0)

        q_raw = sb.tile([P, PACK, Q], F32, name="q_raw")
        k_words = sb.tile([P, 2 * POOL], U8, name="k_words", align_bytes=64)
        n_words = sb.tile([P, POOL], U32, name="n_words", align_bytes=64)
        lam_sb = sb.tile([P, 1], F32, name="lam_sb")
        lists = [sb.tile([P, SLOTS // GROUP], U16, name="list%d" % j) for j in range(5)]

        nc.sync.dma_start(out=q_raw[:], in_=query.rearrange("(p t) q -> p t q", t=PACK))
        load_scale_rows(nc.sync, k_scale, keys_scales, 0)
        load_scale_rows(nc.sync, k_scale, keys_scales, 1)
        load_scale_rows(nc.sync, k_scale, keys_scales, 2)
        load_scale_rows(nc.sync, k_scale, keys_scales, 3)
        nc.sync.dma_start(out=k_words[:].bitcast(I32), in_=keys_words[0].bitcast(I32))
        nc.sync.dma_start(out=n_words[:].bitcast(I32),
                          in_=notes_words[0].rearrange("p n t -> p (n t)").bitcast(I32))
        load_scale_rows(nc.sync, n_scale, notes_scales, 0)
        load_scale_rows(nc.sync, n_scale, notes_scales, 1)
        load_scale_rows(nc.sync, n_scale, notes_scales, 2)
        load_scale_rows(nc.sync, n_scale, notes_scales, 3)
        nc.sync.dma_start(lists[0][:], offs)
        nc.sync.dma_start(lists[1][:], offs2)
        nc.sync.dma_start(lists[2][:], offs3)
        nc.sync.dma_start(lists[3][:], offs4)
        nc.sync.dma_start(lists[4][:], offs5)
        nc.sync.dma_start(out=lam_sb[:], in_=lam)

        q_bf = sb.tile([P, Q, PACK], BF16, name="q_bf", align_bytes=64)
        q_words = sb.tile([P, Q], U32, name="q_words", align_bytes=64)
        q_scale = sb.tile([P, Q], U8, name="q_scale", align_bytes=64)
        nc.vector.tensor_copy(out=q_bf[:, 0:64, :], in_=q_raw[:, :, 0:64].rearrange("p t q -> p q t"))
        nc.scalar.copy(out=q_bf[:, 64:Q, :], in_=q_raw[:, :, 64:Q].rearrange("p t q -> p q t"))
        nc.vector.quantize_mx(out=q_words[:].bitcast(FP8X4), scales=q_scale[:],
                              in_=q_bf[:].rearrange("p q t -> p (q t)"))

        def score(name, moving, scale, widths):
            rows = sb.tile([P, POOL], F32, name=name + "_rows")
            tops = sb.tile([P, len(widths)], F32, name=name + "_tops", tag=name + "_tops")
            neg = sb.tile([P, 1], F32, name=name + "_neg")
            lo = 0
            for j, width in enumerate(widths):
                bank = ps.tile([P, width], F32, name="%s_bank%d" % (name, j))
                nc.tensor.matmul_mx(out=bank[:], lhsT=q_words[:].bitcast(FP8X4), lhsT_scale=q_scale[:],
                                    rhs=moving(lo, lo + width), rhs_scale=scale[:, lo : lo + width],
                                    start=True, stop=True)
                nc.vector.tensor_scalar(out=rows[:, lo : lo + width], in0=bank[:], scalar1=1.0,
                                        scalar2=tops[:, j - 2 : j - 1] if j >= 2 else None,
                                        op0=ALU.mult, op1=ALU.max, accum_out=tops[:, j : j + 1])
                lo = lo + width
            n = len(widths)
            nc.gpsimd.tensor_scalar(out=neg[:], in0=tops[:, n - 2 : n - 1], scalar1=tops[:, n - 1 : n],
                                    scalar2=-1.0, op0=ALU.max, op1=ALU.mult)
            return rows, neg

        a, neg_ta = score("a", lambda lo, hi: k_words[:, 2 * lo : 2 * hi].bitcast(FP4X4), k_scale, (256, 256, 512))
        b, neg_tb = score("b", lambda lo, hi: n_words[:, lo:hi].bitcast(FP8X4), n_scale, (512, 512))

        for h in range(2):
            e1 = sb.tile([P, HALF], F32, name="e1_%d" % h, tag="b_tops" if h == 1 else "e1_first")
            nc.scalar.activation(e1[:], a[:].indirect(half_of_list(lists[0], h)), ACT.Exp, bias=neg_ta[:])
            nc.vector.tensor_copy(f1[:].indirect(half_of_list(lists[2], h)), e1[:])
            e2 = sb.tile([P, HALF], F32, name="e2_%d" % h)
            nc.scalar.activation(e2[:], b[:].indirect(half_of_list(lists[1], h)), ACT.Exp, bias=neg_tb[:])
            nc.vector.tensor_copy(f2[:].indirect(half_of_list(lists[3], h)), e2[:])

        cc = sb.tile([P, PLACES], F32, name="cc")
        nc.vector.scalar_tensor_tensor(out=cc[:], in0=f2[:], scalar=lam_sb[:], in1=f1[:],
                                       op0=ALU.mult, op1=ALU.add)

        y0 = sb.tile([P, 192], F32, name="y0")
        y1 = sb.tile([P, SLOTS - 192], F32, name="y1")
        nc.vector.tensor_tensor(y0[:], cc[:].indirect(lists[4][:, 0 : 192 // GROUP]), eights[:], ALU.mult)
        nc.scalar.activation(y1[:], cc[:].indirect(lists[4][:, 192 // GROUP : SLOTS // GROUP]), ACT.Copy, scale=8.0)
        nc.sync.dma_start(out=out[:, 0:192], in_=y0[:])
        nc.scalar.dma_start(out=out[:, 192:SLOTS], in_=y1[:])
